import numpy as np
import ml_dtypes


def mxq(x, axis, fmt="e4m3"):
    dtype, down = {"e4m3": (ml_dtypes.float8_e4m3fn, 7), "e5m2": (ml_dtypes.float8_e5m2, 14)}[fmt]
    v = np.moveaxis(np.asarray(x, np.float32).astype(ml_dtypes.bfloat16).astype(np.float64), axis, -1)
    blocks = v.reshape(v.shape[:-1] + (-1, 32))
    amax = np.abs(blocks).max(-1, keepdims=True)
    byte = np.maximum(np.where(amax > 0, np.frexp(amax)[1] - 1 + 127, 0) - down, 1)
    scale = np.exp2(byte - 127.0)
    codes = (blocks / scale).astype(np.float32).astype(dtype).astype(np.float64)
    return np.moveaxis((codes * scale).reshape(v.shape), -1, axis)


WIDE = False


def mx_kscale(k):
    if not WIDE:
        return np.ones(k)
    levels = np.array([10, -10, 5, -5, 0])
    if k % 512:
        return np.exp2(np.random.permutation(np.resize(levels, k // 32))).repeat(32)
    a = np.empty((k // 512, 16))
    for p in range(k // 512):
        a[p, :8] = np.random.permutation(np.resize(levels, 8))
        for g in range(8):
            far = levels[np.abs(levels - a[p, g]) >= 10]
            a[p, g + 8] = far[np.random.randint(len(far))]
    return np.exp2(a.ravel()).repeat(32)


def f64(x):
    return np.asarray(x).astype(np.float64)


def striped(idx):
    return np.tile(idx.reshape(-1, 16).T, (8, 1)).astype(np.uint16)


def unstriped(offs):
    return offs[:16].T.reshape(-1).astype(np.int64)


def pack_weight(w):
    k, n = w.shape
    w = f64(np.asarray(w, np.float32).astype(ml_dtypes.bfloat16)).reshape(k // 32, 32, n)
    amax = np.abs(w).max(1)
    byte = np.clip(np.where(amax > 0, np.frexp(amax)[1] - 1 + 127 - 7, 1), 1, 254)
    scaled = (w * np.exp2(127.0 - byte)[:, None, :]).reshape(k, n).astype(np.float32)
    words = np.ascontiguousarray(scaled.reshape(k // 512, 128, 4, n).transpose(0, 1, 3, 2)).astype(ml_dtypes.float8_e4m3fn).view(np.uint8)
    return words, np.ascontiguousarray(byte.astype(np.uint8).reshape(k // 512, 16, n))


def unpack_weight(words, scales):
    g, p, n, _ = words.shape
    vals = np.ascontiguousarray(words).view(ml_dtypes.float8_e4m3fn).astype(np.float64) * np.repeat(np.exp2(scales.astype(np.float64) - 127.0), 8, axis=1)[..., None]
    return vals.transpose(0, 1, 3, 2).reshape(g * 512, n)


K, T, S, N = 1024, 2048, 512, 256
P = 2 ** 7


def setup_inputs():
    n = np.random.standard_normal
    s = mx_kscale(K)[:, None]
    packed_xT = pack_weight(n((K, T)) * s)
    return {
        "x_words": packed_xT[0],
        "x_scales": packed_xT[1],
        "w1": (n((K, N)) / np.sqrt(K) / s).astype(np.float32),
        "w2": (n((K, N)) / np.sqrt(K) / s).astype(np.float32),
        "csd": (np.random.uniform(0.1, 0.6, (N, 1))).astype(np.float32),
        "wall": (np.tile(np.random.uniform(0.2, 1.0, S), (P, 1))).astype(np.float32),
        "offs": striped(np.random.permutation(T)[:S]),
        "east": striped(np.random.permutation(S)),
        "west": striped(np.random.permutation(S)),
        "north": striped(np.random.permutation(S)),
        "south": striped(np.random.permutation(S)),
    }


def reference(x_words, x_scales, w1, w2, csd, wall, offs, east, west, north, south):
    xq = unpack_weight(x_words, x_scales)[:, unstriped(offs)]
    uu = mxq(f64(w1), 0, "e4m3").T @ xq
    ux = 0.5 * (uu[:, unstriped(east)] - uu[:, unstriped(west)])
    vv = mxq(f64(w2), 0, "e4m3").T @ xq
    vy = 0.5 * (vv[:, unstriped(north)] - vv[:, unstriped(south)])
    uy = 0.5 * (uu[:, unstriped(north)] - uu[:, unstriped(south)])
    vx = 0.5 * (vv[:, unstriped(east)] - vv[:, unstriped(west)])
    sxy = 0.5 * (uy + vx)
    smag = np.sqrt(2.0 * ((ux) ** 2 + (vy) ** 2 + 2.0 * ((sxy) ** 2)) + 0.02)
    nut = (f64(csd) * smag) * f64(wall)[:1]
    txy = -2.0 * (nut * sxy)
    return 0.5 * (txy[:, unstriped(north)] - txy[:, unstriped(south)]) + -2.0 * (nut * ux)

@@ -1,0 +1,203 @@
+from contextlib import ExitStack
+
+import concourse.mybir as mybir
+from concourse.masks import make_identity
+
+K, T, S, N = 1024, 2048, 512, 256
+FLOPS = 2 * 2 * K * S * N
+
+F32 = mybir.dt.float32
+BF16 = mybir.dt.bfloat16
+I32 = mybir.dt.int32
+U32 = mybir.dt.uint32
+U16 = mybir.dt.uint16
+U8 = mybir.dt.uint8
+FP8X4 = mybir.dt.float8_e4m3fn_x4
+ALU = mybir.AluOpType
+ACT = mybir.ActivationFunctionType
+
+P = 128
+PACK = 4
+K_PASS = P * PACK
+PASSES = K // K_PASS
+BLOCKS = N // P
+CHUNKS = S // P
+LIST_COLS = S // 16
+WINDOW = S + PACK * N
+HALF = S // 2
+
+
+def tile_picked_yturbo_div_p_kernel(
+    tc, x_words, x_scales, w1, w2, csd, wall, offs, east, west, north, south, out
+):
+    nc = tc.nc
+    with ExitStack() as ctx:
+        lists = ctx.enter_context(tc.tile_pool(name="lists", bufs=1))
+        keep = ctx.enter_context(tc.tile_pool(name="keep", bufs=1))
+        psum = ctx.enter_context(tc.psum_pool(name="psum", bufs=1))
+
+        def sb(shape, dtype, name, tag=None):
+            return keep.tile(shape, dtype, name=name, tag=tag or name, align_bytes=64)
+
+        def load_list(source, name):
+            tile = lists.tile([P, LIST_COLS], U16, name=name, tag=name)
+            nc.sync.dma_start(tile[:], source)
+            return tile
+
+        def load_weight(w, win, o):
+            raw = win[:, S:].rearrange("p (j n) -> p j n", j=PACK)
+            nc.sync.dma_start(raw, w[o * K_PASS : (o + 1) * K_PASS, :].rearrange("(p j) n -> p j n", j=PACK))
+            return raw
+
+        def quantise_weight(raw, name, o):
+            grouped = sb([P, N, PACK], BF16, f"{name}_bf{o}")
+            nc.scalar.copy(
+                grouped[:].rearrange("p (c i) t -> p c t i", i=4),
+                raw.rearrange("p t (c i) -> p c t i", i=4),
+            )
+            codes = sb([P, N], U32, f"{name}_codes{o}")
+            scales = sb([P, N], U8, f"{name}_scales{o}")
+            nc.vector.quantize_mx(
+                out=codes[:].bitcast(FP8X4), scales=scales[:], in_=grouped[:].rearrange("p n t -> p (n t)")
+            )
+            return codes, scales
+
+        scale_table = sb([P, T], U8, "scale_table")
+        nc.gpsimd.memset(scale_table[:].bitcast(I32), 0)
+        offs_t = load_list(offs, "offs")
+        scale_rows = sb([P, T // 4], I32, "scale_rows")
+        for q in range(4):
+            live = slice(32 * q, 32 * q + 4 * PASSES)
+            nc.sync.dma_start(scale_rows[live, :], x_scales[:, 4 * q : 4 * q + 4, :].bitcast(I32))
+            nc.vector.tensor_copy(scale_table[live, :].bitcast(I32), scale_rows[live, :])
+        half = sb([P, 1], F32, "half")
+        nc.vector.memset(half[:], 0.5)
+        root_half = sb([P, 1], F32, "root_half")
+        nc.scalar.activation(root_half[:], half[:], ACT.Sqrt)
+
+        u_win = [sb([P, WINDOW], F32, f"u{b}") for b in range(BLOCKS)]
+        v_win = [sb([P, WINDOW], F32, f"v{b}") for b in range(BLOCKS)]
+        w1_raw = [load_weight(w1, u_win[o], o) for o in range(PASSES)]
+        word_table = []
+        for o in range(PASSES):
+            table = sb([P, T], I32, f"word_table{o}")
+            nc.sync.dma_start(table[:], x_words[o].rearrange("p n t -> p (n t)").bitcast(I32))
+            word_table.append(table)
+        west_t = load_list(west, "west")
+        south_t = load_list(south, "south")
+        east_t = load_list(east, "east")
+        north_t = load_list(north, "north")
+        w2_raw = [load_weight(w2, v_win[o], o) for o in range(PASSES)]
+        csd_t = sb([P, BLOCKS], F32, "csd")
+        wall_t = sb([P, CHUNKS], F32, "wall")
+        with nc.allow_non_contiguous_dma(reason="one value a partition"):
+            nc.sync.dma_start(csd_t[:], csd.rearrange("(b p) o -> p (b o)", p=P))
+            nc.sync.dma_start(wall_t[:], wall[0, :].rearrange("(c p) -> p c", p=P))
+
+        identity = sb([P, P], F32, "identity")
+        make_identity(nc, identity[:])
+
+        x_planes = sb([P, S], U8, "x_planes")
+        nc.vector.tensor_copy(x_planes[:], scale_table[:].indirect(offs_t[:]))
+        w1_q = [quantise_weight(w1_raw[o], "w1", o) for o in range(PASSES)]
+        halves = [(slice(h * HALF, (h + 1) * HALF), slice(h * LIST_COLS // 2, (h + 1) * LIST_COLS // 2)) for h in range(2)]
+        whole = [(slice(0, S), slice(0, LIST_COLS))]
+        x_codes = []
+        for o in range(PASSES):
+            picked = sb([P, S], U32, f"x_codes{o}")
+            for cols, entries in (halves if o == PASSES - 1 else whole):
+                nc.vector.tensor_copy(picked[:, cols], word_table[o][:].bitcast(U32).indirect(offs_t[:, entries]))
+            x_codes.append(picked)
+
+        def product(w_q, b, win, name, cols):
+            acc = psum.tile([P, cols.stop - cols.start], F32, name=name, tag=name)
+            rows = slice(b * P, (b + 1) * P)
+            for o in range(PASSES):
+                codes, scales = w_q[o]
+                nc.tensor.matmul_mx(
+                    out=acc[:],
+                    lhsT=codes[:, rows].bitcast(FP8X4),
+                    lhsT_scale=scales[:, rows],
+                    rhs=x_codes[o][:, cols].bitcast(FP8X4),
+                    rhs_scale=x_planes[4 * o : P, cols],
+                    start=(o == 0),
+                    stop=(o == PASSES - 1),
+                )
+            nc.scalar.copy(win[:, cols], acc[:])
+
+        def fetch(win, lst, name, tag=None):
+            got = sb([P, S], F32, name, tag)
+            nc.vector.tensor_copy(got[:], win[:].indirect(lst[:]))
+            return got
+
+        def fetch_minus(win, lst, other, name):
+            got = sb([P, S], F32, name)
+            nc.vector.tensor_tensor(got[:], win[:].indirect(lst[:]), other[:], ALU.subtract)
+            return got
+
+        def add_square(q_bank, value, scale, name, first, last):
+            sq = sb([P, S], F32, name)
+            nc.scalar.activation(sq[:], value[:], ACT.Square, scale=scale)
+            for c in range(CHUNKS):
+                cols = slice(c * P, (c + 1) * P)
+                nc.tensor.matmul(
+                    q_bank[:, cols], sq[:, cols], identity[:], is_transpose=True,
+                    start=(first and c == 0), stop=(last and c == CHUNKS - 1),
+                )
+
+        for h, (cols, entries) in enumerate(halves):
+            product(w1_q, 0, u_win[0], f"u_bank0{h}", cols)
+        product(w1_q, 1, u_win[1], "u_bank1", slice(0, S))
+
+        q_banks = [psum.tile([P, S], F32, name=f"q_bank{b}", tag=f"q_bank{b}") for b in range(BLOCKS)]
+        du, shear_u = [], []
+
+        def u_part(b, tags):
+            u_w = fetch(u_win[b], west_t, f"u_w{b}", tags[0])
+            u_s = fetch(u_win[b], south_t, f"u_s{b}", tags[1])
+            du.append(fetch_minus(u_win[b], east_t, u_w, f"du{b}"))
+            shear_u.append(fetch_minus(u_win[b], north_t, u_s, f"shear_u{b}"))
+            add_square(q_banks[b], du[b], root_half[:], f"sq_du{b}", True, False)
+
+        u_part(0, (None, None))
+        w2_q = [quantise_weight(w2_raw[o], "w2", o) for o in range(PASSES)]
+        for b in range(BLOCKS):
+            product(w2_q, b, v_win[b], f"v_bank{b}", slice(0, S))
+        u_part(1, ("w2_bf0", "w2_bf1"))
+
+        csd_t4 = sb([P, BLOCKS], F32, "csd_quarter")
+        nc.scalar.mul(csd_t4[:], csd_t[:], -0.25)
+
+        shear, visc = [], []
+        for b in range(BLOCKS):
+            v_s = fetch(v_win[b], south_t, f"v_s{b}")
+            mixed = fetch_minus(v_win[b], west_t, shear_u[b], f"mixed{b}")
+            dv = fetch_minus(v_win[b], north_t, v_s, f"dv{b}")
+            shear.append(fetch_minus(v_win[b], east_t, mixed, f"shear{b}"))
+            add_square(q_banks[b], dv, root_half[:], f"sq_dv{b}", False, False)
+            add_square(q_banks[b], shear[b], 0.5, f"sq_shear{b}", False, True)
+            smag = sb([P, S], F32, f"smag{b}")
+            nc.scalar.activation(smag[:], q_banks[b][:], ACT.Sqrt, bias=0.02)
+            damped = sb([P, S], F32, f"damped{b}")
+            back = psum.tile([P, S], F32, name=f"back{b}", tag=f"u_bank0{b}")
+            for c in range(CHUNKS):
+                cols = slice(c * P, (c + 1) * P)
+                nc.scalar.activation(damped[:, cols], smag[:, cols], ACT.Copy, scale=wall_t[:, c : c + 1])
+                nc.tensor.transpose(back[:, cols], damped[:, cols], identity[:])
+            visc.append(back)
+
+        for b in range(BLOCKS):
+            stress = sb([P, S], F32, f"stress{b}")
+            nc.vector.scalar_tensor_tensor(stress[:], visc[b][:], csd_t4[:, b : b + 1], shear[b][:], ALU.mult, ALU.mult)
+            normal = sb([P, S], F32, f"normal{b}")
+            for cols, entries in halves:
+                nc.vector.scalar_tensor_tensor(
+                    normal[:, cols], visc[b][:, cols], csd_t[:, b : b + 1], du[b][:, cols], ALU.mult, ALU.mult
+                )
+            below = sb([P, S], F32, f"below{b}")
+            for cols, entries in halves:
+                nc.vector.tensor_tensor(below[:, cols], stress[:].indirect(south_t[:, entries]), normal[:, cols], ALU.add)
+            result = sb([P, S], F32, f"result{b}")
+            for cols, entries in halves:
+                nc.vector.tensor_tensor(result[:, cols], stress[:].indirect(north_t[:, entries]), below[:, cols], ALU.subtract)
+                nc.sync.dma_start(out[b * P : (b + 1) * P, cols], result[:, cols])

@@ -23,7 +23,7 @@ PASSES = K // K_PASS
 BLOCKS = N // P
 CHUNKS = S // P
 LIST_COLS = S // 16
-WINDOW = S + PACK * N
+WINDOW = S + PASSES * PACK * P
 HALF = S // 2
 
 
@@ -44,21 +44,24 @@ def tile_picked_yturbo_div_p_kernel(
             nc.sync.dma_start(tile[:], source)
             return tile
 
-        def load_weight(w, win, o):
-            raw = win[:, S:].rearrange("p (j n) -> p j n", j=PACK)
-            nc.sync.dma_start(raw, w[o * K_PASS : (o + 1) * K_PASS, :].rearrange("(p j) n -> p j n", j=PACK))
+        def load_weight(w, b, win):
+            raw = win[:, S:].rearrange("p (o j n) -> p o j n", o=PASSES, j=PACK)
+            for o in range(PASSES):
+                rows = w[o * K_PASS : (o + 1) * K_PASS, b * P : (b + 1) * P]
+                nc.sync.dma_start(raw[:, o], rows.rearrange("(p j) n -> p j n", j=PACK))
             return raw
 
-        def quantise_weight(raw, name, o):
-            grouped = sb([P, N, PACK], BF16, f"{name}_bf{o}")
-            nc.scalar.copy(
-                grouped[:].rearrange("p (c i) t -> p c t i", i=4),
-                raw.rearrange("p t (c i) -> p c t i", i=4),
-            )
-            codes = sb([P, N], U32, f"{name}_codes{o}")
-            scales = sb([P, N], U8, f"{name}_scales{o}")
+        def quantise_weight(raw, name, tag=None):
+            grouped = sb([P, PASSES, P, PACK], BF16, f"{name}_bf", tag)
+            for o in range(PASSES):
+                nc.scalar.copy(
+                    grouped[:, o].rearrange("p (c i) t -> p c t i", i=4),
+                    raw[:, o].rearrange("p t (c i) -> p c t i", i=4),
+                )
+            codes = sb([P, PASSES * P], U32, f"{name}_codes")
+            scales = sb([P, PASSES * P], U8, f"{name}_scales")
             nc.vector.quantize_mx(
-                out=codes[:].bitcast(FP8X4), scales=scales[:], in_=grouped[:].rearrange("p n t -> p (n t)")
+                out=codes[:].bitcast(FP8X4), scales=scales[:], in_=grouped[:].rearrange("p o n t -> p (o n t)")
             )
             return codes, scales
 
@@ -77,7 +80,7 @@ def tile_picked_yturbo_div_p_kernel(
 
         u_win = [sb([P, WINDOW], F32, f"u{b}") for b in range(BLOCKS)]
         v_win = [sb([P, WINDOW], F32, f"v{b}") for b in range(BLOCKS)]
-        w1_raw = [load_weight(w1, u_win[o], o) for o in range(PASSES)]
+        w1_raw = [load_weight(w1, 0, u_win[0])]
         word_table = []
         for o in range(PASSES):
             table = sb([P, T], I32, f"word_table{o}")
@@ -87,7 +90,8 @@ def tile_picked_yturbo_div_p_kernel(
         south_t = load_list(south, "south")
         east_t = load_list(east, "east")
         north_t = load_list(north, "north")
-        w2_raw = [load_weight(w2, v_win[o], o) for o in range(PASSES)]
+        w1_raw.append(load_weight(w1, 1, u_win[1]))
+        w2_raw = [load_weight(w2, b, v_win[b]) for b in range(BLOCKS)]
         csd_t = sb([P, BLOCKS], F32, "csd")
         wall_t = sb([P, CHUNKS], F32, "wall")
         with nc.allow_non_contiguous_dma(reason="one value a partition"):
@@ -99,7 +103,7 @@ def tile_picked_yturbo_div_p_kernel(
 
         x_planes = sb([P, S], U8, "x_planes")
         nc.vector.tensor_copy(x_planes[:], scale_table[:].indirect(offs_t[:]))
-        w1_q = [quantise_weight(w1_raw[o], "w1", o) for o in range(PASSES)]
+        w1_q0 = quantise_weight(w1_raw[0], "w1_0")
         halves = [(slice(h * HALF, (h + 1) * HALF), slice(h * LIST_COLS // 2, (h + 1) * LIST_COLS // 2)) for h in range(2)]
         whole = [(slice(0, S), slice(0, LIST_COLS))]
         x_codes = []
@@ -109,11 +113,11 @@ def tile_picked_yturbo_div_p_kernel(
                 nc.vector.tensor_copy(picked[:, cols], word_table[o][:].bitcast(U32).indirect(offs_t[:, entries]))
             x_codes.append(picked)
 
-        def product(w_q, b, win, name, cols):
+        def product(w_q, win, name, cols):
             acc = psum.tile([P, cols.stop - cols.start], F32, name=name, tag=name)
-            rows = slice(b * P, (b + 1) * P)
+            codes, scales = w_q
             for o in range(PASSES):
-                codes, scales = w_q[o]
+                rows = slice(o * P, (o + 1) * P)
                 nc.tensor.matmul_mx(
                     out=acc[:],
                     lhsT=codes[:, rows].bitcast(FP8X4),
@@ -130,40 +134,43 @@ def tile_picked_yturbo_div_p_kernel(
             nc.vector.tensor_copy(got[:], win[:].indirect(lst[:]))
             return got
 
-        def fetch_minus(win, lst, other, name):
-            got = sb([P, S], F32, name)
-            nc.vector.tensor_tensor(got[:], win[:].indirect(lst[:]), other[:], ALU.subtract)
+        def fetch_minus(win, lst, other, name, pieces, tag=None):
+            got = sb([P, S], F32, name, tag)
+            for cols, entries in pieces:
+                nc.vector.tensor_tensor(got[:, cols], win[:].indirect(lst[:, entries]), other[:, cols], ALU.subtract)
             return got
 
-        def add_square(q_bank, value, scale, name, first, last):
-            sq = sb([P, S], F32, name)
-            nc.scalar.activation(sq[:], value[:], ACT.Square, scale=scale)
-            for c in range(CHUNKS):
+        def add_square(q_bank, value, h, scale, name, first, last):
+            sq = sb([P, HALF], F32, f"{name}_{h}")
+            nc.scalar.activation(sq[:], value[:, halves[h][0]], ACT.Square, scale=scale)
+            for c in range(CHUNKS // 2):
                 cols = slice(c * P, (c + 1) * P)
                 nc.tensor.matmul(
                     q_bank[:, cols], sq[:, cols], identity[:], is_transpose=True,
-                    start=(first and c == 0), stop=(last and c == CHUNKS - 1),
+                    start=(first and c == 0), stop=(last and c == CHUNKS // 2 - 1),
                 )
 
         for h, (cols, entries) in enumerate(halves):
-            product(w1_q, 0, u_win[0], f"u_bank0{h}", cols)
-        product(w1_q, 1, u_win[1], "u_bank1", slice(0, S))
+            product(w1_q0, u_win[0], f"u_bank0{h}", cols)
+        product(quantise_weight(w1_raw[1], "w1_1", "w1_0_codes"), u_win[1], "u_bank1", slice(0, S))
+        for b in range(BLOCKS):
+            product(quantise_weight(w2_raw[b], f"w2_{b}"), v_win[b], f"v_bank{b}", slice(0, S))
 
-        q_banks = [psum.tile([P, S], F32, name=f"q_bank{b}", tag=f"q_bank{b}") for b in range(BLOCKS)]
+        q_tags = [["u_bank00", "u_bank01"], ["u_bank1", "v_bank0"]]
+        q_banks = []
         du, shear_u = [], []
 
         def u_part(b, tags):
             u_w = fetch(u_win[b], west_t, f"u_w{b}", tags[0])
-            u_s = fetch(u_win[b], south_t, f"u_s{b}", tags[1])
-            du.append(fetch_minus(u_win[b], east_t, u_w, f"du{b}"))
-            shear_u.append(fetch_minus(u_win[b], north_t, u_s, f"shear_u{b}"))
-            add_square(q_banks[b], du[b], root_half[:], f"sq_du{b}", True, False)
+            u_s = fetch(u_win[b], south_t, f"u_s{b}")
+            du.append(fetch_minus(u_win[b], east_t, u_w, f"du{b}", whole, tags[1]))
+            shear_u.append(fetch_minus(u_win[b], north_t, u_s, f"shear_u{b}", whole))
+            q_banks.append([psum.tile([P, HALF], F32, name=f"q_bank{b}{h}", tag=q_tags[b][h]) for h in range(2)])
+            for h in range(2):
+                add_square(q_banks[b][h], du[b], h, root_half[:], f"sq_du{b}", True, False)
 
-        u_part(0, (None, None))
-        w2_q = [quantise_weight(w2_raw[o], "w2", o) for o in range(PASSES)]
-        for b in range(BLOCKS):
-            product(w2_q, b, v_win[b], f"v_bank{b}", slice(0, S))
-        u_part(1, ("w2_bf0", "w2_bf1"))
+        u_part(0, (None, "w1_0_codes"))
+        u_part(1, ("w2_0_bf", "w2_1_bf"))
 
         csd_t4 = sb([P, BLOCKS], F32, "csd_quarter")
         nc.scalar.mul(csd_t4[:], csd_t[:], -0.25)
@@ -171,19 +178,23 @@ def tile_picked_yturbo_div_p_kernel(
         shear, visc = [], []
         for b in range(BLOCKS):
             v_s = fetch(v_win[b], south_t, f"v_s{b}")
-            mixed = fetch_minus(v_win[b], west_t, shear_u[b], f"mixed{b}")
-            dv = fetch_minus(v_win[b], north_t, v_s, f"dv{b}")
-            shear.append(fetch_minus(v_win[b], east_t, mixed, f"shear{b}"))
-            add_square(q_banks[b], dv, root_half[:], f"sq_dv{b}", False, False)
-            add_square(q_banks[b], shear[b], 0.5, f"sq_shear{b}", False, True)
-            smag = sb([P, S], F32, f"smag{b}")
-            nc.scalar.activation(smag[:], q_banks[b][:], ACT.Sqrt, bias=0.02)
-            damped = sb([P, S], F32, f"damped{b}")
-            back = psum.tile([P, S], F32, name=f"back{b}", tag=f"u_bank0{b}")
-            for c in range(CHUNKS):
-                cols = slice(c * P, (c + 1) * P)
-                nc.scalar.activation(damped[:, cols], smag[:, cols], ACT.Copy, scale=wall_t[:, c : c + 1])
-                nc.tensor.transpose(back[:, cols], damped[:, cols], identity[:])
+            mixed = fetch_minus(v_win[b], west_t, shear_u[b], f"mixed{b}", whole)
+            dv = fetch_minus(v_win[b], north_t, v_s, f"dv{b}", whole)
+            shear.append(fetch_minus(v_win[b], east_t, mixed, f"shear{b}", halves))
+            for h in range(2):
+                add_square(q_banks[b][h], dv, h, root_half[:], f"sq_dv{b}", False, False)
+            for h in range(2):
+                add_square(q_banks[b][h], shear[b], h, 0.5, f"sq_shear{b}", False, True)
+            back = psum.tile([P, S], F32, name=f"back{b}", tag=f"back{b}")
+            for h in range(2):
+                smag = sb([P, HALF], F32, f"smag{b}{h}")
+                nc.scalar.activation(smag[:], q_banks[b][h][:], ACT.Sqrt, bias=0.02)
+                damped = sb([P, HALF], F32, f"damped{b}{h}")
+                for i in range(CHUNKS // 2):
+                    c = h * CHUNKS // 2 + i
+                    cols = slice(i * P, (i + 1) * P)
+                    nc.scalar.activation(damped[:, cols], smag[:, cols], ACT.Copy, scale=wall_t[:, c : c + 1])
+                    nc.tensor.transpose(back[:, c * P : (c + 1) * P], damped[:, cols], identity[:])
             visc.append(back)
 
         for b in range(BLOCKS):

@@ -44,17 +44,19 @@ def tile_picked_yturbo_div_p_kernel(
             nc.sync.dma_start(tile[:], source)
             return tile
 
-        def load_weight(w, b, win):
-            raw = win[:, S:].rearrange("p (o j n) -> p o j n", o=PASSES, j=PACK)
-            for o in range(PASSES):
-                rows = w[o * K_PASS : (o + 1) * K_PASS, b * P : (b + 1) * P]
-                nc.sync.dma_start(raw[:, o], rows.rearrange("(p j) n -> p j n", j=PACK))
-            return raw
+        def spare(win):
+            return win[:, S:].rearrange("p (o j n) -> p o j n", o=PASSES, j=PACK)
 
-        def quantise_weight(raw, name, tag=None):
-            grouped = sb([P, PASSES, P, PACK], BF16, f"{name}_bf", tag)
+        def load_weight(w, b, win, passes=range(PASSES)):
+            for o in passes:
+                rows = w[o * K_PASS : (o + 1) * K_PASS, b * P : (b + 1) * P]
+                nc.sync.dma_start(spare(win)[:, o], rows.rearrange("(p j) n -> p j n", j=PACK))
+            return spare(win)
+
+        def quantise_weight(raw, name, cast):
+            grouped = sb([P, PASSES, P, PACK], BF16, f"{name}_bf")
             for o in range(PASSES):
-                nc.scalar.copy(
+                cast(
                     grouped[:, o].rearrange("p (c i) t -> p c t i", i=4),
                     raw[:, o].rearrange("p t (c i) -> p c t i", i=4),
                 )
@@ -65,32 +67,33 @@ def tile_picked_yturbo_div_p_kernel(
             )
             return codes, scales
 
+        u_win = [sb([P, WINDOW], F32, f"u{b}") for b in range(BLOCKS)]
+        v_win = [sb([P, WINDOW], F32, f"v{b}") for b in range(BLOCKS)]
+        load_weight(w1, 0, u_win[0], [0])
         scale_table = sb([P, T], U8, "scale_table")
         nc.gpsimd.memset(scale_table[:].bitcast(I32), 0)
-        offs_t = load_list(offs, "offs")
         scale_rows = sb([P, T // 4], I32, "scale_rows")
         for q in range(4):
             live = slice(32 * q, 32 * q + 4 * PASSES)
             nc.sync.dma_start(scale_rows[live, :], x_scales[:, 4 * q : 4 * q + 4, :].bitcast(I32))
             nc.vector.tensor_copy(scale_table[live, :].bitcast(I32), scale_rows[live, :])
+        offs_t = load_list(offs, "offs")
         half = sb([P, 1], F32, "half")
         nc.vector.memset(half[:], 0.5)
         root_half = sb([P, 1], F32, "root_half")
         nc.scalar.activation(root_half[:], half[:], ACT.Sqrt)
 
-        u_win = [sb([P, WINDOW], F32, f"u{b}") for b in range(BLOCKS)]
-        v_win = [sb([P, WINDOW], F32, f"v{b}") for b in range(BLOCKS)]
-        w1_raw = [load_weight(w1, 0, u_win[0])]
+        w1_raw = [load_weight(w1, 0, u_win[0], [1])]
         word_table = []
         for o in range(PASSES):
             table = sb([P, T], I32, f"word_table{o}")
             nc.sync.dma_start(table[:], x_words[o].rearrange("p n t -> p (n t)").bitcast(I32))
             word_table.append(table)
+        w1_raw.append(load_weight(w1, 1, u_win[1]))
         west_t = load_list(west, "west")
         south_t = load_list(south, "south")
         east_t = load_list(east, "east")
         north_t = load_list(north, "north")
-        w1_raw.append(load_weight(w1, 1, u_win[1]))
         w2_raw = [load_weight(w2, b, v_win[b]) for b in range(BLOCKS)]
         csd_t = sb([P, BLOCKS], F32, "csd")
         wall_t = sb([P, CHUNKS], F32, "wall")
@@ -103,7 +106,7 @@ def tile_picked_yturbo_div_p_kernel(
 
         x_planes = sb([P, S], U8, "x_planes")
         nc.vector.tensor_copy(x_planes[:], scale_table[:].indirect(offs_t[:]))
-        w1_q0 = quantise_weight(w1_raw[0], "w1_0")
+        w1_q0 = quantise_weight(w1_raw[0], "w1_0", nc.scalar.copy)
         halves = [(slice(h * HALF, (h + 1) * HALF), slice(h * LIST_COLS // 2, (h + 1) * LIST_COLS // 2)) for h in range(2)]
         whole = [(slice(0, S), slice(0, LIST_COLS))]
         x_codes = []
@@ -152,9 +155,9 @@ def tile_picked_yturbo_div_p_kernel(
 
         for h, (cols, entries) in enumerate(halves):
             product(w1_q0, u_win[0], f"u_bank0{h}", cols)
-        product(quantise_weight(w1_raw[1], "w1_1", "w1_0_codes"), u_win[1], "u_bank1", slice(0, S))
+        product(quantise_weight(w1_raw[1], "w1_1", nc.vector.tensor_copy), u_win[1], "u_bank1", slice(0, S))
         for b in range(BLOCKS):
-            product(quantise_weight(w2_raw[b], f"w2_{b}"), v_win[b], f"v_bank{b}", slice(0, S))
+            product(quantise_weight(w2_raw[b], f"w2_{b}", nc.scalar.copy), v_win[b], f"v_bank{b}", slice(0, S))
 
         q_tags = [["u_bank00", "u_bank01"], ["u_bank1", "v_bank0"]]
         q_banks = []
@@ -169,7 +172,7 @@ def tile_picked_yturbo_div_p_kernel(
             for h in range(2):
                 add_square(q_banks[b][h], du[b], h, root_half[:], f"sq_du{b}", True, False)
 
-        u_part(0, (None, "w1_0_codes"))
+        u_part(0, (None, None))
         u_part(1, ("w2_0_bf", "w2_1_bf"))
 
         csd_t4 = sb([P, BLOCKS], F32, "csd_quarter")

@@ -21,10 +21,23 @@ PACK = 4
 K_PASS = P * PACK
 PASSES = K // K_PASS
 BLOCKS = N // P
-CHUNKS = S // P
+QUADRANT = 32
+SCALE_ROWS = 4
 LIST_COLS = S // 16
-WINDOW = S + PASSES * PACK * P
 HALF = S // 2
+HALF_CHUNKS = HALF // P
+LINE = 4
+WINDOW = S + PASSES * PACK * P
+
+
+def pieces(count):
+    cells, entries = S // count, LIST_COLS // count
+    return [(slice(i * cells, (i + 1) * cells), slice(i * entries, (i + 1) * entries)) for i in range(count)]
+
+
+WHOLE = pieces(1)
+HALVES = pieces(2)
+TAPERED = HALVES[:1] + pieces(4)[2:]
 
 
 def tile_picked_yturbo_div_p_kernel(
@@ -44,21 +57,20 @@ def tile_picked_yturbo_div_p_kernel(
             nc.sync.dma_start(tile[:], source)
             return tile
 
-        def spare(win):
-            return win[:, S:].rearrange("p (o j n) -> p o j n", o=PASSES, j=PACK)
+        def raw_weights(win):
+            return win[:, S:].rearrange("p (o t n) -> p o t n", o=PASSES, t=PACK)
 
-        def load_weight(w, b, win, passes=range(PASSES)):
+        def load_weights(w, b, win, passes):
             for o in passes:
                 rows = w[o * K_PASS : (o + 1) * K_PASS, b * P : (b + 1) * P]
-                nc.sync.dma_start(spare(win)[:, o], rows.rearrange("(p j) n -> p j n", j=PACK))
-            return spare(win)
+                nc.sync.dma_start(raw_weights(win)[:, o], rows.rearrange("(p t) n -> p t n", t=PACK))
 
-        def quantise_weight(raw, name, cast):
+        def quantise_weights(win, name, cast):
             grouped = sb([P, PASSES, P, PACK], BF16, f"{name}_bf")
             for o in range(PASSES):
                 cast(
-                    grouped[:, o].rearrange("p (c i) t -> p c t i", i=4),
-                    raw[:, o].rearrange("p t (c i) -> p c t i", i=4),
+                    grouped[:, o].rearrange("p (c i) t -> p c t i", i=LINE),
+                    raw_weights(win)[:, o].rearrange("p t (c i) -> p c t i", i=LINE),
                 )
             codes = sb([P, PASSES * P], U32, f"{name}_codes")
             scales = sb([P, PASSES * P], U8, f"{name}_scales")
@@ -69,34 +81,38 @@ def tile_picked_yturbo_div_p_kernel(
 
         u_win = [sb([P, WINDOW], F32, f"u{b}") for b in range(BLOCKS)]
         v_win = [sb([P, WINDOW], F32, f"v{b}") for b in range(BLOCKS)]
-        load_weight(w1, 0, u_win[0], [0])
+        load_weights(w1, 0, u_win[0], [0])
+
         scale_table = sb([P, T], U8, "scale_table")
         nc.gpsimd.memset(scale_table[:].bitcast(I32), 0)
         scale_rows = sb([P, T // 4], I32, "scale_rows")
-        for q in range(4):
-            live = slice(32 * q, 32 * q + 4 * PASSES)
-            nc.sync.dma_start(scale_rows[live, :], x_scales[:, 4 * q : 4 * q + 4, :].bitcast(I32))
+        for q in range(P // QUADRANT):
+            live = slice(QUADRANT * q, QUADRANT * q + SCALE_ROWS * PASSES)
+            rows = x_scales[:, SCALE_ROWS * q : SCALE_ROWS * (q + 1), :]
+            nc.sync.dma_start(scale_rows[live, :], rows.bitcast(I32))
             nc.vector.tensor_copy(scale_table[live, :].bitcast(I32), scale_rows[live, :])
         offs_t = load_list(offs, "offs")
-        half = sb([P, 1], F32, "half")
-        nc.vector.memset(half[:], 0.5)
-        root_half = sb([P, 1], F32, "root_half")
-        nc.scalar.activation(root_half[:], half[:], ACT.Sqrt)
 
-        w1_raw = [load_weight(w1, 0, u_win[0], [1])]
+        one_half = sb([P, 1], F32, "one_half")
+        nc.vector.memset(one_half[:], 0.5)
+        root_half = sb([P, 1], F32, "root_half")
+        nc.scalar.activation(root_half[:], one_half[:], ACT.Sqrt)
+
+        load_weights(w1, 0, u_win[0], [1])
         word_table = []
         for o in range(PASSES):
             table = sb([P, T], I32, f"word_table{o}")
             nc.sync.dma_start(table[:], x_words[o].rearrange("p n t -> p (n t)").bitcast(I32))
             word_table.append(table)
-        w1_raw.append(load_weight(w1, 1, u_win[1]))
+        load_weights(w1, 1, u_win[1], range(PASSES))
         west_t = load_list(west, "west")
         south_t = load_list(south, "south")
         east_t = load_list(east, "east")
         north_t = load_list(north, "north")
-        w2_raw = [load_weight(w2, b, v_win[b]) for b in range(BLOCKS)]
+        for b in range(BLOCKS):
+            load_weights(w2, b, v_win[b], range(PASSES))
         csd_t = sb([P, BLOCKS], F32, "csd")
-        wall_t = sb([P, CHUNKS], F32, "wall")
+        wall_t = sb([P, S // P], F32, "wall")
         with nc.allow_non_contiguous_dma(reason="one value a partition"):
             nc.sync.dma_start(csd_t[:], csd.rearrange("(b p) o -> p (b o)", p=P))
             nc.sync.dma_start(wall_t[:], wall[0, :].rearrange("(c p) -> p c", p=P))
@@ -106,19 +122,17 @@ def tile_picked_yturbo_div_p_kernel(
 
         x_planes = sb([P, S], U8, "x_planes")
         nc.vector.tensor_copy(x_planes[:], scale_table[:].indirect(offs_t[:]))
-        w1_q0 = quantise_weight(w1_raw[0], "w1_0", nc.scalar.copy)
-        halves = [(slice(h * HALF, (h + 1) * HALF), slice(h * LIST_COLS // 2, (h + 1) * LIST_COLS // 2)) for h in range(2)]
-        whole = [(slice(0, S), slice(0, LIST_COLS))]
+        w1_first = quantise_weights(u_win[0], "w1_0", nc.scalar.copy)
         x_codes = []
         for o in range(PASSES):
             picked = sb([P, S], U32, f"x_codes{o}")
-            for cols, entries in (halves if o == PASSES - 1 else whole):
+            for cols, entries in HALVES if o == PASSES - 1 else WHOLE:
                 nc.vector.tensor_copy(picked[:, cols], word_table[o][:].bitcast(U32).indirect(offs_t[:, entries]))
             x_codes.append(picked)
 
-        def product(w_q, win, name, cols):
-            acc = psum.tile([P, cols.stop - cols.start], F32, name=name, tag=name)
-            codes, scales = w_q
+        def product(quantised, win, bank, cols):
+            acc = psum.tile([P, cols.stop - cols.start], F32, name=bank, tag=bank)
+            codes, scales = quantised
             for o in range(PASSES):
                 rows = slice(o * P, (o + 1) * P)
                 nc.tensor.matmul_mx(
@@ -126,7 +140,7 @@ def tile_picked_yturbo_div_p_kernel(
                     lhsT=codes[:, rows].bitcast(FP8X4),
                     lhsT_scale=scales[:, rows],
                     rhs=x_codes[o][:, cols].bitcast(FP8X4),
-                    rhs_scale=x_planes[4 * o : P, cols],
+                    rhs_scale=x_planes[SCALE_ROWS * o : P, cols],
                     start=(o == 0),
                     stop=(o == PASSES - 1),
                 )
@@ -137,81 +151,87 @@ def tile_picked_yturbo_div_p_kernel(
             nc.vector.tensor_copy(got[:], win[:].indirect(lst[:]))
             return got
 
-        def fetch_minus(win, lst, other, name, pieces, tag=None):
+        def fetch_minus(win, lst, other, name, runs=WHOLE, tag=None):
             got = sb([P, S], F32, name, tag)
-            for cols, entries in pieces:
+            for cols, entries in runs:
                 nc.vector.tensor_tensor(got[:, cols], win[:].indirect(lst[:, entries]), other[:, cols], ALU.subtract)
             return got
 
-        def add_square(q_bank, value, h, scale, name, first, last):
-            sq = sb([P, HALF], F32, f"{name}_{h}")
-            nc.scalar.activation(sq[:], value[:, halves[h][0]], ACT.Square, scale=scale)
-            for c in range(CHUNKS // 2):
-                cols = slice(c * P, (c + 1) * P)
-                nc.tensor.matmul(
-                    q_bank[:, cols], sq[:, cols], identity[:], is_transpose=True,
-                    start=(first and c == 0), stop=(last and c == CHUNKS // 2 - 1),
-                )
+        def add_square(banks, value, scale, name, first=False, last=False):
+            for h, (cols, entries) in enumerate(HALVES):
+                square = sb([P, HALF], F32, f"{name}_{h}")
+                nc.scalar.activation(square[:], value[:, cols], ACT.Square, scale=scale)
+                for c in range(HALF_CHUNKS):
+                    chunk = slice(c * P, (c + 1) * P)
+                    nc.tensor.matmul(
+                        banks[h][:, chunk],
+                        square[:, chunk],
+                        identity[:],
+                        is_transpose=True,
+                        start=(first and c == 0),
+                        stop=(last and c == HALF_CHUNKS - 1),
+                    )
 
-        for h, (cols, entries) in enumerate(halves):
-            product(w1_q0, u_win[0], f"u_bank0{h}", cols)
-        product(quantise_weight(w1_raw[1], "w1_1", nc.vector.tensor_copy), u_win[1], "u_bank1", slice(0, S))
+        for h, (cols, entries) in enumerate(HALVES):
+            product(w1_first, u_win[0], f"u_bank0{h}", cols)
+        product(quantise_weights(u_win[1], "w1_1", nc.vector.tensor_copy), u_win[1], "u_bank1", slice(0, S))
         for b in range(BLOCKS):
-            product(quantise_weight(w2_raw[b], f"w2_{b}", nc.scalar.copy), v_win[b], f"v_bank{b}", slice(0, S))
+            product(quantise_weights(v_win[b], f"w2_{b}", nc.scalar.copy), v_win[b], f"v_bank{b}", slice(0, S))
 
-        q_tags = [["u_bank00", "u_bank01"], ["u_bank1", "v_bank0"]]
-        q_banks = []
-        du, shear_u = [], []
-
-        def u_part(b, tags):
-            u_w = fetch(u_win[b], west_t, f"u_w{b}", tags[0])
-            u_s = fetch(u_win[b], south_t, f"u_s{b}")
-            du.append(fetch_minus(u_win[b], east_t, u_w, f"du{b}", whole, tags[1]))
-            shear_u.append(fetch_minus(u_win[b], north_t, u_s, f"shear_u{b}", whole))
-            q_banks.append([psum.tile([P, HALF], F32, name=f"q_bank{b}{h}", tag=q_tags[b][h]) for h in range(2)])
-            for h in range(2):
-                add_square(q_banks[b][h], du[b], h, root_half[:], f"sq_du{b}", True, False)
-
-        u_part(0, (None, None))
-        u_part(1, ("w2_0_bf", "w2_1_bf"))
-
-        csd_t4 = sb([P, BLOCKS], F32, "csd_quarter")
-        nc.scalar.mul(csd_t4[:], csd_t[:], -0.25)
-
-        shear, visc = [], []
+        square_tags = [["u_bank00", "u_bank01"], ["u_bank1", "v_bank0"]]
+        reused = [(None, None), ("w2_0_bf", "w2_1_bf")]
+        square_banks, du, shear_u = [], [], []
         for b in range(BLOCKS):
-            v_s = fetch(v_win[b], south_t, f"v_s{b}")
-            mixed = fetch_minus(v_win[b], west_t, shear_u[b], f"mixed{b}", whole)
-            dv = fetch_minus(v_win[b], north_t, v_s, f"dv{b}", whole)
-            shear.append(fetch_minus(v_win[b], east_t, mixed, f"shear{b}", halves))
-            for h in range(2):
-                add_square(q_banks[b][h], dv, h, root_half[:], f"sq_dv{b}", False, False)
-            for h in range(2):
-                add_square(q_banks[b][h], shear[b], h, 0.5, f"sq_shear{b}", False, True)
-            back = psum.tile([P, S], F32, name=f"back{b}", tag=f"back{b}")
-            for h in range(2):
-                smag = sb([P, HALF], F32, f"smag{b}{h}")
-                nc.scalar.activation(smag[:], q_banks[b][h][:], ACT.Sqrt, bias=0.02)
-                damped = sb([P, HALF], F32, f"damped{b}{h}")
-                for i in range(CHUNKS // 2):
-                    c = h * CHUNKS // 2 + i
-                    cols = slice(i * P, (i + 1) * P)
-                    nc.scalar.activation(damped[:, cols], smag[:, cols], ACT.Copy, scale=wall_t[:, c : c + 1])
-                    nc.tensor.transpose(back[:, c * P : (c + 1) * P], damped[:, cols], identity[:])
-            visc.append(back)
+            u_west = fetch(u_win[b], west_t, f"u_west{b}", reused[b][0])
+            u_south = fetch(u_win[b], south_t, f"u_south{b}")
+            du.append(fetch_minus(u_win[b], east_t, u_west, f"du{b}", tag=reused[b][1]))
+            shear_u.append(fetch_minus(u_win[b], north_t, u_south, f"shear_u{b}"))
+            square_banks.append(
+                [psum.tile([P, HALF], F32, name=f"squares{b}{h}", tag=square_tags[b][h]) for h in range(len(HALVES))]
+            )
+            add_square(square_banks[b], du[b], root_half[:], f"du_square{b}", first=True)
+
+        stress_factor = sb([P, BLOCKS], F32, "stress_factor")
+        nc.scalar.mul(stress_factor[:], csd_t[:], -0.25)
+
+        shear, damped = [], []
+        for b in range(BLOCKS):
+            v_south = fetch(v_win[b], south_t, f"v_south{b}")
+            partial = fetch_minus(v_win[b], west_t, shear_u[b], f"partial{b}")
+            dv = fetch_minus(v_win[b], north_t, v_south, f"dv{b}")
+            shear.append(fetch_minus(v_win[b], east_t, partial, f"shear{b}", HALVES if b == BLOCKS - 1 else WHOLE))
+            add_square(square_banks[b], dv, root_half[:], f"dv_square{b}")
+            add_square(square_banks[b], shear[b], 0.5, f"shear_square{b}", last=True)
+            back = psum.tile([P, S], F32, name=f"damped{b}", tag=f"damped{b}")
+            for h in range(len(HALVES)):
+                smag_t = sb([P, HALF], F32, f"smag_t{b}{h}")
+                nc.scalar.activation(smag_t[:], square_banks[b][h][:], ACT.Sqrt, bias=0.02)
+                damped_t = sb([P, HALF], F32, f"damped_t{b}{h}")
+                for i in range(HALF_CHUNKS):
+                    c = h * HALF_CHUNKS + i
+                    chunk = slice(i * P, (i + 1) * P)
+                    nc.scalar.activation(damped_t[:, chunk], smag_t[:, chunk], ACT.Copy, scale=wall_t[:, c : c + 1])
+                    nc.tensor.transpose(back[:, c * P : (c + 1) * P], damped_t[:, chunk], identity[:])
+            damped.append(back)
 
         for b in range(BLOCKS):
             stress = sb([P, S], F32, f"stress{b}")
-            nc.vector.scalar_tensor_tensor(stress[:], visc[b][:], csd_t4[:, b : b + 1], shear[b][:], ALU.mult, ALU.mult)
-            normal = sb([P, S], F32, f"normal{b}")
-            for cols, entries in halves:
+            nc.vector.scalar_tensor_tensor(
+                stress[:], damped[b][:], stress_factor[:, b : b + 1], shear[b][:], ALU.mult, ALU.mult
+            )
+            nut_du = sb([P, S], F32, f"nut_du{b}")
+            for cols, entries in HALVES:
                 nc.vector.scalar_tensor_tensor(
-                    normal[:, cols], visc[b][:, cols], csd_t[:, b : b + 1], du[b][:, cols], ALU.mult, ALU.mult
+                    nut_du[:, cols], damped[b][:, cols], csd_t[:, b : b + 1], du[b][:, cols], ALU.mult, ALU.mult
                 )
-            below = sb([P, S], F32, f"below{b}")
-            for cols, entries in halves:
-                nc.vector.tensor_tensor(below[:, cols], stress[:].indirect(south_t[:, entries]), normal[:, cols], ALU.add)
+            subtrahend = sb([P, S], F32, f"subtrahend{b}")
+            for cols, entries in HALVES:
+                nc.vector.tensor_tensor(
+                    subtrahend[:, cols], stress[:].indirect(south_t[:, entries]), nut_du[:, cols], ALU.add
+                )
             result = sb([P, S], F32, f"result{b}")
-            for cols, entries in halves:
-                nc.vector.tensor_tensor(result[:, cols], stress[:].indirect(north_t[:, entries]), below[:, cols], ALU.subtract)
+            for cols, entries in TAPERED if b == BLOCKS - 1 else HALVES:
+                nc.vector.tensor_tensor(
+                    result[:, cols], stress[:].indirect(north_t[:, entries]), subtrahend[:, cols], ALU.subtract
+                )
                 nc.sync.dma_start(out[b * P : (b + 1) * P, cols], result[:, cols])

from contextlib import ExitStack

import concourse.mybir as mybir
from concourse.masks import make_identity

K, T, S, N = 1024, 2048, 512, 256
FLOPS = 2 * 2 * K * S * N

F32 = mybir.dt.float32
BF16 = mybir.dt.bfloat16
I32 = mybir.dt.int32
U32 = mybir.dt.uint32
U16 = mybir.dt.uint16
U8 = mybir.dt.uint8
FP8X4 = mybir.dt.float8_e4m3fn_x4
ALU = mybir.AluOpType
ACT = mybir.ActivationFunctionType

P = 128
PACK = 4
K_PASS = P * PACK
PASSES = K // K_PASS
BLOCKS = N // P
QUADRANT = 32
SCALE_ROWS = 4
LIST_COLS = S // 16
HALF = S // 2
HALF_CHUNKS = HALF // P
LINE = 4
WINDOW = S + PASSES * PACK * P


def pieces(count):
    cells, entries = S // count, LIST_COLS // count
    return [(slice(i * cells, (i + 1) * cells), slice(i * entries, (i + 1) * entries)) for i in range(count)]


WHOLE = pieces(1)
HALVES = pieces(2)
TAPERED = HALVES[:1] + pieces(4)[2:]


def tile_picked_yturbo_div_p_kernel(
    tc, x_words, x_scales, w1, w2, csd, wall, offs, east, west, north, south, out
):
    nc = tc.nc
    with ExitStack() as ctx:
        lists = ctx.enter_context(tc.tile_pool(name="lists", bufs=1))
        keep = ctx.enter_context(tc.tile_pool(name="keep", bufs=1))
        psum = ctx.enter_context(tc.psum_pool(name="psum", bufs=1))

        def sb(shape, dtype, name, tag=None):
            return keep.tile(shape, dtype, name=name, tag=tag or name, align_bytes=64)

        def load_list(source, name):
            tile = lists.tile([P, LIST_COLS], U16, name=name, tag=name)
            nc.sync.dma_start(tile[:], source)
            return tile

        def raw_weights(win):
            return win[:, S:].rearrange("p (o t n) -> p o t n", o=PASSES, t=PACK)

        def load_weights(w, b, win, passes):
            for o in passes:
                rows = w[o * K_PASS : (o + 1) * K_PASS, b * P : (b + 1) * P]
                nc.sync.dma_start(raw_weights(win)[:, o], rows.rearrange("(p t) n -> p t n", t=PACK))

        def quantise_weights(win, name, cast):
            grouped = sb([P, PASSES, P, PACK], BF16, f"{name}_bf")
            for o in range(PASSES):
                cast(
                    grouped[:, o].rearrange("p (c i) t -> p c t i", i=LINE),
                    raw_weights(win)[:, o].rearrange("p t (c i) -> p c t i", i=LINE),
                )
            codes = sb([P, PASSES * P], U32, f"{name}_codes")
            scales = sb([P, PASSES * P], U8, f"{name}_scales")
            nc.vector.quantize_mx(
                out=codes[:].bitcast(FP8X4), scales=scales[:], in_=grouped[:].rearrange("p o n t -> p (o n t)")
            )
            return codes, scales

        u_win = [sb([P, WINDOW], F32, f"u{b}") for b in range(BLOCKS)]
        v_win = [sb([P, WINDOW], F32, f"v{b}") for b in range(BLOCKS)]
        load_weights(w1, 0, u_win[0], [0])

        scale_table = sb([P, T], U8, "scale_table")
        nc.gpsimd.memset(scale_table[:].bitcast(I32), 0)
        scale_rows = sb([P, T // 4], I32, "scale_rows")
        for q in range(P // QUADRANT):
            live = slice(QUADRANT * q, QUADRANT * q + SCALE_ROWS * PASSES)
            rows = x_scales[:, SCALE_ROWS * q : SCALE_ROWS * (q + 1), :]
            nc.sync.dma_start(scale_rows[live, :], rows.bitcast(I32))
            nc.vector.tensor_copy(scale_table[live, :].bitcast(I32), scale_rows[live, :])
        offs_t = load_list(offs, "offs")

        one_half = sb([P, 1], F32, "one_half")
        nc.vector.memset(one_half[:], 0.5)
        root_half = sb([P, 1], F32, "root_half")
        nc.scalar.activation(root_half[:], one_half[:], ACT.Sqrt)

        load_weights(w1, 0, u_win[0], [1])
        word_table = []
        for o in range(PASSES):
            table = sb([P, T], I32, f"word_table{o}")
            nc.sync.dma_start(table[:], x_words[o].rearrange("p n t -> p (n t)").bitcast(I32))
            word_table.append(table)
        load_weights(w1, 1, u_win[1], range(PASSES))
        west_t = load_list(west, "west")
        south_t = load_list(south, "south")
        east_t = load_list(east, "east")
        north_t = load_list(north, "north")
        for b in range(BLOCKS):
            load_weights(w2, b, v_win[b], range(PASSES))
        csd_t = sb([P, BLOCKS], F32, "csd")
        wall_t = sb([P, S // P], F32, "wall")
        with nc.allow_non_contiguous_dma(reason="one value a partition"):
            nc.sync.dma_start(csd_t[:], csd.rearrange("(b p) o -> p (b o)", p=P))
            nc.sync.dma_start(wall_t[:], wall[0, :].rearrange("(c p) -> p c", p=P))

        identity = sb([P, P], F32, "identity")
        make_identity(nc, identity[:])

        x_planes = sb([P, S], U8, "x_planes")
        nc.vector.tensor_copy(x_planes[:], scale_table[:].indirect(offs_t[:]))
        w1_first = quantise_weights(u_win[0], "w1_0", nc.scalar.copy)
        x_codes = []
        for o in range(PASSES):
            picked = sb([P, S], U32, f"x_codes{o}")
            for cols, entries in HALVES if o == PASSES - 1 else WHOLE:
                nc.vector.tensor_copy(picked[:, cols], word_table[o][:].bitcast(U32).indirect(offs_t[:, entries]))
            x_codes.append(picked)

        def product(quantised, win, bank, cols):
            acc = psum.tile([P, cols.stop - cols.start], F32, name=bank, tag=bank)
            codes, scales = quantised
            for o in range(PASSES):
                rows = slice(o * P, (o + 1) * P)
                nc.tensor.matmul_mx(
                    out=acc[:],
                    lhsT=codes[:, rows].bitcast(FP8X4),
                    lhsT_scale=scales[:, rows],
                    rhs=x_codes[o][:, cols].bitcast(FP8X4),
                    rhs_scale=x_planes[SCALE_ROWS * o : P, cols],
                    start=(o == 0),
                    stop=(o == PASSES - 1),
                )
            nc.scalar.copy(win[:, cols], acc[:])

        def fetch(win, lst, name, tag=None):
            got = sb([P, S], F32, name, tag)
            nc.vector.tensor_copy(got[:], win[:].indirect(lst[:]))
            return got

        def fetch_minus(win, lst, other, name, runs=WHOLE, tag=None):
            got = sb([P, S], F32, name, tag)
            for cols, entries in runs:
                nc.vector.tensor_tensor(got[:, cols], win[:].indirect(lst[:, entries]), other[:, cols], ALU.subtract)
            return got

        def add_square(banks, value, scale, name, first=False, last=False):
            for h, (cols, entries) in enumerate(HALVES):
                square = sb([P, HALF], F32, f"{name}_{h}")
                nc.scalar.activation(square[:], value[:, cols], ACT.Square, scale=scale)
                for c in range(HALF_CHUNKS):
                    chunk = slice(c * P, (c + 1) * P)
                    nc.tensor.matmul(
                        banks[h][:, chunk],
                        square[:, chunk],
                        identity[:],
                        is_transpose=True,
                        start=(first and c == 0),
                        stop=(last and c == HALF_CHUNKS - 1),
                    )

        for h, (cols, entries) in enumerate(HALVES):
            product(w1_first, u_win[0], f"u_bank0{h}", cols)
        product(quantise_weights(u_win[1], "w1_1", nc.vector.tensor_copy), u_win[1], "u_bank1", slice(0, S))
        for b in range(BLOCKS):
            product(quantise_weights(v_win[b], f"w2_{b}", nc.scalar.copy), v_win[b], f"v_bank{b}", slice(0, S))

        square_tags = [["u_bank00", "u_bank01"], ["u_bank1", "v_bank0"]]
        reused = [(None, None), ("w2_0_bf", "w2_1_bf")]
        square_banks, du, shear_u = [], [], []
        for b in range(BLOCKS):
            u_west = fetch(u_win[b], west_t, f"u_west{b}", reused[b][0])
            u_south = fetch(u_win[b], south_t, f"u_south{b}")
            du.append(fetch_minus(u_win[b], east_t, u_west, f"du{b}", tag=reused[b][1]))
            shear_u.append(fetch_minus(u_win[b], north_t, u_south, f"shear_u{b}"))
            square_banks.append(
                [psum.tile([P, HALF], F32, name=f"squares{b}{h}", tag=square_tags[b][h]) for h in range(len(HALVES))]
            )
            add_square(square_banks[b], du[b], root_half[:], f"du_square{b}", first=True)

        stress_factor = sb([P, BLOCKS], F32, "stress_factor")
        nc.scalar.mul(stress_factor[:], csd_t[:], -0.25)

        shear, damped = [], []
        for b in range(BLOCKS):
            v_south = fetch(v_win[b], south_t, f"v_south{b}")
            partial = fetch_minus(v_win[b], west_t, shear_u[b], f"partial{b}")
            dv = fetch_minus(v_win[b], north_t, v_south, f"dv{b}")
            shear.append(fetch_minus(v_win[b], east_t, partial, f"shear{b}", HALVES if b == BLOCKS - 1 else WHOLE))
            add_square(square_banks[b], dv, root_half[:], f"dv_square{b}")
            add_square(square_banks[b], shear[b], 0.5, f"shear_square{b}", last=True)
            back = psum.tile([P, S], F32, name=f"damped{b}", tag=f"damped{b}")
            for h in range(len(HALVES)):
                smag_t = sb([P, HALF], F32, f"smag_t{b}{h}")
                nc.scalar.activation(smag_t[:], square_banks[b][h][:], ACT.Sqrt, bias=0.02)
                damped_t = sb([P, HALF], F32, f"damped_t{b}{h}")
                for i in range(HALF_CHUNKS):
                    c = h * HALF_CHUNKS + i
                    chunk = slice(i * P, (i + 1) * P)
                    nc.scalar.activation(damped_t[:, chunk], smag_t[:, chunk], ACT.Copy, scale=wall_t[:, c : c + 1])
                    nc.tensor.transpose(back[:, c * P : (c + 1) * P], damped_t[:, chunk], identity[:])
            damped.append(back)

        for b in range(BLOCKS):
            stress = sb([P, S], F32, f"stress{b}")
            nc.vector.scalar_tensor_tensor(
                stress[:], damped[b][:], stress_factor[:, b : b + 1], shear[b][:], ALU.mult, ALU.mult
            )
            nut_du = sb([P, S], F32, f"nut_du{b}")
            for cols, entries in HALVES:
                nc.vector.scalar_tensor_tensor(
                    nut_du[:, cols], damped[b][:, cols], csd_t[:, b : b + 1], du[b][:, cols], ALU.mult, ALU.mult
                )
            subtrahend = sb([P, S], F32, f"subtrahend{b}")
            for cols, entries in HALVES:
                nc.vector.tensor_tensor(
                    subtrahend[:, cols], stress[:].indirect(south_t[:, entries]), nut_du[:, cols], ALU.add
                )
            result = sb([P, S], F32, f"result{b}")
            for cols, entries in TAPERED if b == BLOCKS - 1 else HALVES:
                nc.vector.tensor_tensor(
                    result[:, cols], stress[:].indirect(north_t[:, entries]), subtrahend[:, cols], ALU.subtract
                )
                nc.sync.dma_start(out[b * P : (b + 1) * P, cols], result[:, cols])
